import numpy as np
CORES = [32,33,40,41,48,49,56,57,64,65,72,73]
N = 12
def setup_inputs(rng):
    return {"x": rng.standard_normal((N, 128, 1024), dtype=np.float32)}
def reference(x):
    s = x.sum(axis=0, dtype=np.float64).astype(x.dtype)
    return {"y": np.broadcast_to(s, (N,) + s.shape)}

@@ -1,0 +1,122 @@
+from concourse.bass import DstId, RemoteDMATransfer
+
+U = (43, 43, 42)
+W = (344, 344, 336)
+C0 = (0, 344, 688)
+PORTS = (2, 3, 6, 7)
+FIRST_CHIP = 4
+
+SCRATCH = {}
+for _t in range(3):
+    SCRATCH["X%d" % _t] = ("dram", [8, 128, U[_t]], "float32")
+    SCRATCH["R%d" % _t] = ("dram", [8, 128, U[_t]], "float32")
+    SCRATCH["L%d" % _t] = ("dram", [4, 128, U[_t]], "float32")
+    SCRATCH["M%d" % _t] = ("dram", [128, U[_t]], "float32")
+    SCRATCH["P%d" % _t] = ("dram", [2, 128, U[_t]], "float32")
+
+SEMAPHORES = (["ld%d" % i for i in range(6)] + ["lf%d" % t for t in range(3)] + ["ln%d" % t for t in range(3)]
+              + ["m%d" % t for t in range(3)] + ["f%d" % t for t in range(3)] + ["n%d" % t for t in range(3)]
+              + ["s%d" % t for t in range(3)] + ["p", "sent", "stn", "stf"])
+
+
+def _dst(topo, core):
+    rid, pid, _se = topo.addr(core)
+    return DstId(rid=rid, pnc=pid)
+
+
+def _rank(g, core, T, topo):
+    ch, i = topo.chip(core), core % 8
+    near = ch & 1
+    far = 1 - near
+    j = (ch - FIRST_CHIP) // 2
+    order = [j] + [t for t in range(3) if t != j]
+    queues = (g, g.sync, g.scalar)
+    sent = 0
+    for k, h in enumerate((far, near)):
+        for t in range(3):
+            queues[t].dma_start(T["X%d" % t][4 * h:4 * h + 4],
+                                T.x[64 * h:64 * h + 64, C0[t]:C0[t] + W[t]]).then_inc(T.sem["ld%d" % (3 * k + t)], 16)
+    for k, h in enumerate((far, near)):
+        for t in range(3):
+            g.wait_ge(T.sem["ld%d" % (3 * k + t)], 16)
+            g.remote_dma_fused([
+                RemoteDMATransfer(dst_ids=[_dst(topo, ch * 8 + PORTS[q])], dma_engine_mask=0xF << (4 * q),
+                                  remote_sem=T.sem[("lf%d" if h == far else "ln%d") % t],
+                                  src=T["X%d" % t][4 * h + q], dst=T["L%d" % t][2 * (h == far) + i])
+                for q in range(4)], local_sem=T.sem.sent)
+            sent += 16
+    for t in order:
+        g.wait_ge(T.sem["f%d" % t], 16)
+        g.remote_dma_fused([
+            RemoteDMATransfer(dst_ids=[_dst(topo, core ^ 1)], dma_engine_mask=0xFF << (8 * e),
+                              remote_sem=T.sem["s%d" % t],
+                              src=T["R%d" % t][4 * far + i + 2 * e], dst=T["R%d" % t][4 * far + i + 2 * e])
+            for e in range(2)], local_sem=T.sem.sent)
+        sent += 16
+    for t in order:
+        g.sync.wait_ge(T.sem["n%d" % t], 32)
+        g.sync.dma_start(T.y[64 * near:64 * near + 64, C0[t]:C0[t] + W[t]],
+                         T["R%d" % t][4 * near:4 * near + 4]).then_inc(T.sem.stn, 16)
+        g.scalar.wait_ge(T.sem["f%d" % t], 16)
+        g.scalar.wait_ge(T.sem["s%d" % t], 16)
+        g.scalar.dma_start(T.y[64 * far:64 * far + 64, C0[t]:C0[t] + W[t]],
+                           T["R%d" % t][4 * far:4 * far + 4]).then_inc(T.sem.stf, 16)
+    g.wait_ge(T.sem.sent, sent)
+    g.wait_ge(T.sem.stn, 48)
+    g.wait_ge(T.sem.stf, 48)
+
+
+def _port(g, core, T, topo):
+    ch, k = topo.chip(core), core % 8
+    q = PORTS.index(k)
+    p = ch & 1
+    j = (ch - FIRST_CHIP) // 2
+    others = [t for t in range(3) if t != j]
+    b = 4 * p + q
+    mate_port = _dst(topo, (ch ^ 1) * 8 + k)
+    mate_rank = _dst(topo, (ch ^ 1) * 8 + q % 2)
+    ranks = [_dst(topo, ch * 8), _dst(topo, ch * 8 + 1)]
+    plane = [_dst(topo, (FIRST_CHIP + 2 * t + p) * 8 + k) for t in range(3)]
+    sent = 0
+    for t in range(3):
+        g.wait_ge(T.sem["lf%d" % t], 8)
+        g.remote_dma_fused([RemoteDMATransfer(dst_ids=[mate_port], dma_engine_mask=0xFF, remote_sem=T.sem["m%d" % t],
+                                              srcs=[T["L%d" % t][2], T["L%d" % t][3]], dsts=[T["M%d" % t][:]],
+                                              alu_op=1)], local_sem=T.sem.sent)
+        sent += 8
+    for t in others:
+        g.wait_ge(T.sem["ln%d" % t], 8)
+        g.wait_ge(T.sem["m%d" % t], 8)
+        slot = [c for c in range(3) if c != t].index(j)
+        g.remote_dma_fused([RemoteDMATransfer(dst_ids=[plane[t]], dma_engine_mask=0xFF, remote_sem=T.sem.p,
+                                              srcs=[T["L%d" % t][0], T["L%d" % t][1], T["M%d" % t][:]],
+                                              dsts=[T["P%d" % t][slot]], alu_op=1)], local_sem=T.sem.sent)
+        sent += 8
+    g.wait_ge(T.sem["ln%d" % j], 8)
+    g.wait_ge(T.sem["m%d" % j], 8)
+    g.wait_ge(T.sem.p, 16)
+    srcs = [T["L%d" % j][0], T["L%d" % j][1], T["M%d" % j][:], T["P%d" % j][0], T["P%d" % j][1]]
+    piece = T["R%d" % j][b]
+    g.remote_dma_fused([
+        RemoteDMATransfer(dst_ids=[plane[others[0]], plane[others[1]], mate_rank], dma_engine_mask=0x00FF,
+                          remote_sem=T.sem["f%d" % j], srcs=srcs, dsts=[piece, piece, piece], alu_op=1),
+        RemoteDMATransfer(dst_ids=ranks, dma_engine_mask=0xFF00, remote_sem=T.sem["n%d" % j],
+                          srcs=srcs, dsts=[piece, piece], alu_op=1)], local_sem=T.sem.sent)
+    sent += 16
+    for t in others:
+        g.wait_ge(T.sem["f%d" % t], 8)
+        piece = T["R%d" % t][b]
+        g.remote_dma_fused([
+            RemoteDMATransfer(dst_ids=[mate_rank], dma_engine_mask=0x00FF, remote_sem=T.sem["f%d" % t],
+                              srcs=[piece], dsts=[piece]),
+            RemoteDMATransfer(dst_ids=ranks, dma_engine_mask=0xFF00, remote_sem=T.sem["n%d" % t],
+                              srcs=[piece], dsts=[piece, piece])], local_sem=T.sem.sent)
+        sent += 16
+    g.wait_ge(T.sem.sent, sent)
+
+
+def rank_program(g, core, T, topo):
+    if T.rank_of(core) is not None:
+        _rank(g, core, T, topo)
+    elif FIRST_CHIP <= topo.chip(core) < FIRST_CHIP + 6 and core % 8 in PORTS:
+        _port(g, core, T, topo)

@@ -1,122 +1,146 @@
 from concourse.bass import DstId, RemoteDMATransfer
 
-U = (43, 43, 42)
-W = (344, 344, 336)
-C0 = (0, 344, 688)
 PORTS = (2, 3, 6, 7)
-FIRST_CHIP = 4
+NB, NS = 4, 6
+RB, RS = 23, 6
+UB, US = 2 * RB, 2 * RS
+S0 = NB * RB
+ADD = 1
 
-SCRATCH = {}
-for _t in range(3):
-    SCRATCH["X%d" % _t] = ("dram", [8, 128, U[_t]], "float32")
-    SCRATCH["R%d" % _t] = ("dram", [8, 128, U[_t]], "float32")
-    SCRATCH["L%d" % _t] = ("dram", [4, 128, U[_t]], "float32")
-    SCRATCH["M%d" % _t] = ("dram", [128, U[_t]], "float32")
-    SCRATCH["P%d" % _t] = ("dram", [2, 128, U[_t]], "float32")
+SCRATCH = {
+    "XB": ("dram", [4 * NB, 128, UB], "float32"),
+    "XS": ("dram", [4 * NS, 128, US], "float32"),
+    "LB": ("dram", [2 * NB, 128, UB], "float32"),
+    "LS": ("dram", [2 * NS, 128, US], "float32"),
+    "PB": ("dram", [6, 128, UB], "float32"),
+    "PS": ("dram", [6, 128, US], "float32"),
+    "YB": ("dram", [4 * NB, 128, UB], "float32"),
+    "YS": ("dram", [4 * NS, 128, US], "float32"),
+}
+SEMAPHORES = (["ld%d" % k for k in range(5)]
+              + ["lb%d" % b for b in range(NB)] + ["ls"]
+              + ["pb", "ps"]
+              + ["fb%d" % b for b in range(NB)] + ["fs"]
+              + ["nb%d" % b for b in range(NB)] + ["ns"]
+              + ["sent", "stg", "sta", "stb"])
 
-SEMAPHORES = (["ld%d" % i for i in range(6)] + ["lf%d" % t for t in range(3)] + ["ln%d" % t for t in range(3)]
-              + ["m%d" % t for t in range(3)] + ["f%d" % t for t in range(3)] + ["n%d" % t for t in range(3)]
-              + ["s%d" % t for t in range(3)] + ["p", "sent", "stn", "stf"])
 
-
-def _dst(topo, core):
+def _id(topo, core):
     rid, pid, _se = topo.addr(core)
     return DstId(rid=rid, pnc=pid)
 
 
+def _copy(topo, cores, mask, sem, src, dst):
+    return RemoteDMATransfer(dst_ids=[_id(topo, c) for c in cores], dma_engine_mask=mask, remote_sem=sem,
+                             srcs=[src], dsts=[dst] * len(cores))
+
+
+def _fold(topo, cores, mask, sem, srcs, dst):
+    return RemoteDMATransfer(dst_ids=[_id(topo, c) for c in cores], dma_engine_mask=mask, remote_sem=sem,
+                             srcs=srcs, dsts=[dst] * len(cores), alu_op=ADD)
+
+
+def _waves(parity):
+    return (parity, 1 - parity, 2 + parity, 3 - parity)
+
+
 def _rank(g, core, T, topo):
     ch, i = topo.chip(core), core % 8
-    near = ch & 1
-    far = 1 - near
-    j = (ch - FIRST_CHIP) // 2
-    order = [j] + [t for t in range(3) if t != j]
-    queues = (g, g.sync, g.scalar)
+    order = _waves(ch & 1)
+    ports = [ch * 8 + k for k in PORTS]
     sent = 0
-    for k, h in enumerate((far, near)):
-        for t in range(3):
-            queues[t].dma_start(T["X%d" % t][4 * h:4 * h + 4],
-                                T.x[64 * h:64 * h + 64, C0[t]:C0[t] + W[t]]).then_inc(T.sem["ld%d" % (3 * k + t)], 16)
-    for k, h in enumerate((far, near)):
-        for t in range(3):
-            g.wait_ge(T.sem["ld%d" % (3 * k + t)], 16)
-            g.remote_dma_fused([
-                RemoteDMATransfer(dst_ids=[_dst(topo, ch * 8 + PORTS[q])], dma_engine_mask=0xF << (4 * q),
-                                  remote_sem=T.sem[("lf%d" if h == far else "ln%d") % t],
-                                  src=T["X%d" % t][4 * h + q], dst=T["L%d" % t][2 * (h == far) + i])
-                for q in range(4)], local_sem=T.sem.sent)
-            sent += 16
-    for t in order:
-        g.wait_ge(T.sem["f%d" % t], 16)
-        g.remote_dma_fused([
-            RemoteDMATransfer(dst_ids=[_dst(topo, core ^ 1)], dma_engine_mask=0xFF << (8 * e),
-                              remote_sem=T.sem["s%d" % t],
-                              src=T["R%d" % t][4 * far + i + 2 * e], dst=T["R%d" % t][4 * far + i + 2 * e])
-            for e in range(2)], local_sem=T.sem.sent)
+    g.sync.dma_start(T.XS[:], T.x[S0:128, :]).then_inc(T.sem.ld4, 16)
+    for k, b in enumerate(order):
+        (g.scalar, g.sync)[k % 2].dma_start(T.XB[4 * b:4 * b + 4],
+                                            T.x[RB * b:RB * (b + 1), :]).then_inc(T.sem["ld%d" % k], 16)
+    g.wait_ge(T.sem.ld4, 16)
+    g.remote_dma_fused([_copy(topo, [ports[q]], 1 << (4 * s + q), T.sem.ls, T.XS[4 * s + q], T.LS[2 * s + i])
+                        for s in range(4) for q in range(4)], local_sem=T.sem.sent)
+    g.remote_dma_fused([_copy(topo, [ports[q]], 3 << (2 * (4 * (s - 4) + q)), T.sem.ls, T.XS[4 * s + q],
+                              T.LS[2 * s + i])
+                        for s in range(4, 6) for q in range(4)], local_sem=T.sem.sent)
+    sent += 32
+    for k, b in enumerate(order):
+        g.wait_ge(T.sem["ld%d" % k], 16)
+        g.remote_dma_fused([_copy(topo, [ports[q]], 0xF << (4 * q), T.sem["lb%d" % b], T.XB[4 * b + q],
+                                  T.LB[2 * b + i]) for q in range(4)], local_sem=T.sem.sent)
         sent += 16
-    for t in order:
-        g.sync.wait_ge(T.sem["n%d" % t], 32)
-        g.sync.dma_start(T.y[64 * near:64 * near + 64, C0[t]:C0[t] + W[t]],
-                         T["R%d" % t][4 * near:4 * near + 4]).then_inc(T.sem.stn, 16)
-        g.scalar.wait_ge(T.sem["f%d" % t], 16)
-        g.scalar.wait_ge(T.sem["s%d" % t], 16)
-        g.scalar.dma_start(T.y[64 * far:64 * far + 64, C0[t]:C0[t] + W[t]],
-                           T["R%d" % t][4 * far:4 * far + 4]).then_inc(T.sem.stf, 16)
+    g.wait_ge(T.sem.ns, 4 * 4 + 2 * 10)
+    g.dma_start(T.y[S0:128, :], T.YS[:]).then_inc(T.sem.stg, 16)
+    for k, b in enumerate(order):
+        qu, sem = ((g.sync, T.sem.sta), (g.scalar, T.sem.stb))[k % 2]
+        qu.wait_ge(T.sem["nb%d" % b], 4 * 8)
+        qu.dma_start(T.y[RB * b:RB * (b + 1), :], T.YB[4 * b:4 * b + 4]).then_inc(sem, 16)
+    g.wait_ge(T.sem.stg, 16)
     g.wait_ge(T.sem.sent, sent)
-    g.wait_ge(T.sem.stn, 48)
-    g.wait_ge(T.sem.stf, 48)
+    g.wait_ge(T.sem.sta, 32)
+    g.wait_ge(T.sem.stb, 32)
 
 
 def _port(g, core, T, topo):
     ch, k = topo.chip(core), core % 8
     q = PORTS.index(k)
-    p = ch & 1
-    j = (ch - FIRST_CHIP) // 2
-    others = [t for t in range(3) if t != j]
-    b = 4 * p + q
-    mate_port = _dst(topo, (ch ^ 1) * 8 + k)
-    mate_rank = _dst(topo, (ch ^ 1) * 8 + q % 2)
-    ranks = [_dst(topo, ch * 8), _dst(topo, ch * 8 + 1)]
-    plane = [_dst(topo, (FIRST_CHIP + 2 * t + p) * 8 + k) for t in range(3)]
+    me = ch - NB
+    others = [(me + d) % NS for d in range(1, NS)]
+    order = _waves(ch & 1)
+    ranks = (ch * 8, ch * 8 + 1)
     sent = 0
-    for t in range(3):
-        g.wait_ge(T.sem["lf%d" % t], 8)
-        g.remote_dma_fused([RemoteDMATransfer(dst_ids=[mate_port], dma_engine_mask=0xFF, remote_sem=T.sem["m%d" % t],
-                                              srcs=[T["L%d" % t][2], T["L%d" % t][3]], dsts=[T["M%d" % t][:]],
-                                              alu_op=1)], local_sem=T.sem.sent)
+    g.wait_ge(T.sem.ls, 16)
+    g.remote_dma_fused([_fold(topo, [(NB + s) * 8 + k], 1 << e, T.sem.ps, [T.LS[2 * s], T.LS[2 * s + 1]], T.PS[me])
+                        for e, s in enumerate(others)], local_sem=T.sem.sent)
+    sent += 5
+    for b in order:
+        g.wait_ge(T.sem["lb%d" % b], 8)
+        g.remote_dma_fused([_fold(topo, [b * 8 + k], 0xFF, T.sem.pb, [T.LB[2 * b], T.LB[2 * b + 1]], T.PB[me])],
+                           local_sem=T.sem.sent)
         sent += 8
-    for t in others:
-        g.wait_ge(T.sem["ln%d" % t], 8)
-        g.wait_ge(T.sem["m%d" % t], 8)
-        slot = [c for c in range(3) if c != t].index(j)
-        g.remote_dma_fused([RemoteDMATransfer(dst_ids=[plane[t]], dma_engine_mask=0xFF, remote_sem=T.sem.p,
-                                              srcs=[T["L%d" % t][0], T["L%d" % t][1], T["M%d" % t][:]],
-                                              dsts=[T["P%d" % t][slot]], alu_op=1)], local_sem=T.sem.sent)
-        sent += 8
-    g.wait_ge(T.sem["ln%d" % j], 8)
-    g.wait_ge(T.sem["m%d" % j], 8)
-    g.wait_ge(T.sem.p, 16)
-    srcs = [T["L%d" % j][0], T["L%d" % j][1], T["M%d" % j][:], T["P%d" % j][0], T["P%d" % j][1]]
-    piece = T["R%d" % j][b]
-    g.remote_dma_fused([
-        RemoteDMATransfer(dst_ids=[plane[others[0]], plane[others[1]], mate_rank], dma_engine_mask=0x00FF,
-                          remote_sem=T.sem["f%d" % j], srcs=srcs, dsts=[piece, piece, piece], alu_op=1),
-        RemoteDMATransfer(dst_ids=ranks, dma_engine_mask=0xFF00, remote_sem=T.sem["n%d" % j],
-                          srcs=srcs, dsts=[piece, piece], alu_op=1)], local_sem=T.sem.sent)
-    sent += 16
-    for t in others:
-        g.wait_ge(T.sem["f%d" % t], 8)
-        piece = T["R%d" % t][b]
-        g.remote_dma_fused([
-            RemoteDMATransfer(dst_ids=[mate_rank], dma_engine_mask=0x00FF, remote_sem=T.sem["f%d" % t],
-                              srcs=[piece], dsts=[piece]),
-            RemoteDMATransfer(dst_ids=ranks, dma_engine_mask=0xFF00, remote_sem=T.sem["n%d" % t],
-                              srcs=[piece], dsts=[piece, piece])], local_sem=T.sem.sent)
+    g.wait_ge(T.sem.ps, 5)
+    srcs = [T.LS[2 * me], T.LS[2 * me + 1]] + [T.PS[s] for s in others]
+    piece = T.YS[4 * me + q]
+    g.remote_dma_fused([_fold(topo, [(NB + s) * 8 + 4 + q % 2], 1 << e, T.sem.fs, srcs, piece)
+                        for e, s in enumerate(others)]
+                       + [_fold(topo, [ranks[r]], 0xF00 << (4 * r), T.sem.ns, srcs, piece) for r in range(2)],
+                       local_sem=T.sem.sent)
+    sent += 5 + 8
+    for b in order:
+        g.wait_ge(T.sem["fb%d" % b], 4)
+        piece = T.YB[4 * b + q]
+        g.remote_dma_fused([_copy(topo, [ranks[r]], 0xFF << (8 * r), T.sem["nb%d" % b], piece, piece)
+                            for r in range(2)], local_sem=T.sem.sent)
         sent += 16
     g.wait_ge(T.sem.sent, sent)
 
 
+def _passer(g, core, T, topo):
+    ch, i = topo.chip(core), core % 8 - 4
+    me = ch - NB
+    pieces = [4 * s + q for s in range(NS) if s != me for q in (i, i + 2)]
+    g.wait_ge(T.sem.fs, 10)
+    g.remote_dma_fused([_copy(topo, [ch * 8, ch * 8 + 1], 1 << e, T.sem.ns, T.YS[n], T.YS[n])
+                        for e, n in enumerate(pieces)], local_sem=T.sem.sent)
+    g.wait_ge(T.sem.sent, 10)
+
+
+def _owner(g, core, T, topo):
+    b, k = topo.chip(core), core % 8
+    q = PORTS.index(k)
+    srcs = [T.PB[s] for s in range(NS)]
+    piece = T.YB[4 * b + q]
+    g.wait_ge(T.sem.pb, 6 * 8)
+    g.remote_dma_fused([_fold(topo, [c * 8 + k for c in range(NB, NB + NS) if (c + b + par) % 2 == 1],
+                              0xF << (4 * par), T.sem["fb%d" % b], srcs, piece) for par in range(2)],
+                       local_sem=T.sem.sent)
+    g.wait_ge(T.sem.sent, 8)
+
+
 def rank_program(g, core, T, topo):
+    ch, k = topo.chip(core), core % 8
     if T.rank_of(core) is not None:
         _rank(g, core, T, topo)
-    elif FIRST_CHIP <= topo.chip(core) < FIRST_CHIP + 6 and core % 8 in PORTS:
+    elif ch < NB:
+        if k in PORTS:
+            _owner(g, core, T, topo)
+    elif k in PORTS:
         _port(g, core, T, topo)
+    else:
+        _passer(g, core, T, topo)

from concourse.bass import DstId, RemoteDMATransfer

PORTS = (2, 3, 6, 7)
NB, NS = 4, 6
RB, RS = 23, 6
UB, US = 2 * RB, 2 * RS
S0 = NB * RB
ADD = 1

SCRATCH = {
    "XB": ("dram", [4 * NB, 128, UB], "float32"),
    "XS": ("dram", [4 * NS, 128, US], "float32"),
    "LB": ("dram", [2 * NB, 128, UB], "float32"),
    "LS": ("dram", [2 * NS, 128, US], "float32"),
    "PB": ("dram", [6, 128, UB], "float32"),
    "PS": ("dram", [6, 128, US], "float32"),
    "YB": ("dram", [4 * NB, 128, UB], "float32"),
    "YS": ("dram", [4 * NS, 128, US], "float32"),
}
SEMAPHORES = (["ld%d" % k for k in range(5)]
              + ["lb%d" % b for b in range(NB)] + ["ls"]
              + ["pb", "ps"]
              + ["fb%d" % b for b in range(NB)] + ["fs"]
              + ["nb%d" % b for b in range(NB)] + ["ns"]
              + ["sent", "stg", "sta", "stb"])


def _id(topo, core):
    rid, pid, _se = topo.addr(core)
    return DstId(rid=rid, pnc=pid)


def _copy(topo, cores, mask, sem, src, dst):
    return RemoteDMATransfer(dst_ids=[_id(topo, c) for c in cores], dma_engine_mask=mask, remote_sem=sem,
                             srcs=[src], dsts=[dst] * len(cores))


def _fold(topo, cores, mask, sem, srcs, dst):
    return RemoteDMATransfer(dst_ids=[_id(topo, c) for c in cores], dma_engine_mask=mask, remote_sem=sem,
                             srcs=srcs, dsts=[dst] * len(cores), alu_op=ADD)


def _waves(parity):
    return (parity, 1 - parity, 2 + parity, 3 - parity)


def _rank(g, core, T, topo):
    ch, i = topo.chip(core), core % 8
    order = _waves(ch & 1)
    ports = [ch * 8 + k for k in PORTS]
    sent = 0
    g.sync.dma_start(T.XS[:], T.x[S0:128, :]).then_inc(T.sem.ld4, 16)
    for k, b in enumerate(order):
        (g.scalar, g.sync)[k % 2].dma_start(T.XB[4 * b:4 * b + 4],
                                            T.x[RB * b:RB * (b + 1), :]).then_inc(T.sem["ld%d" % k], 16)
    g.wait_ge(T.sem.ld4, 16)
    g.remote_dma_fused([_copy(topo, [ports[q]], 1 << (4 * s + q), T.sem.ls, T.XS[4 * s + q], T.LS[2 * s + i])
                        for s in range(4) for q in range(4)], local_sem=T.sem.sent)
    g.remote_dma_fused([_copy(topo, [ports[q]], 3 << (2 * (4 * (s - 4) + q)), T.sem.ls, T.XS[4 * s + q],
                              T.LS[2 * s + i])
                        for s in range(4, 6) for q in range(4)], local_sem=T.sem.sent)
    sent += 32
    for k, b in enumerate(order):
        g.wait_ge(T.sem["ld%d" % k], 16)
        g.remote_dma_fused([_copy(topo, [ports[q]], 0xF << (4 * q), T.sem["lb%d" % b], T.XB[4 * b + q],
                                  T.LB[2 * b + i]) for q in range(4)], local_sem=T.sem.sent)
        sent += 16
    g.wait_ge(T.sem.ns, 4 * 4 + 2 * 10)
    g.dma_start(T.y[S0:128, :], T.YS[:]).then_inc(T.sem.stg, 16)
    for k, b in enumerate(order):
        qu, sem = ((g.sync, T.sem.sta), (g.scalar, T.sem.stb))[k % 2]
        qu.wait_ge(T.sem["nb%d" % b], 4 * 8)
        qu.dma_start(T.y[RB * b:RB * (b + 1), :], T.YB[4 * b:4 * b + 4]).then_inc(sem, 16)
    g.wait_ge(T.sem.stg, 16)
    g.wait_ge(T.sem.sent, sent)
    g.wait_ge(T.sem.sta, 32)
    g.wait_ge(T.sem.stb, 32)


def _port(g, core, T, topo):
    ch, k = topo.chip(core), core % 8
    q = PORTS.index(k)
    me = ch - NB
    others = [(me + d) % NS for d in range(1, NS)]
    order = _waves(ch & 1)
    ranks = (ch * 8, ch * 8 + 1)
    sent = 0
    g.wait_ge(T.sem.ls, 16)
    g.remote_dma_fused([_fold(topo, [(NB + s) * 8 + k], 1 << e, T.sem.ps, [T.LS[2 * s], T.LS[2 * s + 1]], T.PS[me])
                        for e, s in enumerate(others)], local_sem=T.sem.sent)
    sent += 5
    for b in order:
        g.wait_ge(T.sem["lb%d" % b], 8)
        g.remote_dma_fused([_fold(topo, [b * 8 + k], 0xFF, T.sem.pb, [T.LB[2 * b], T.LB[2 * b + 1]], T.PB[me])],
                           local_sem=T.sem.sent)
        sent += 8
    g.wait_ge(T.sem.ps, 5)
    srcs = [T.LS[2 * me], T.LS[2 * me + 1]] + [T.PS[s] for s in others]
    piece = T.YS[4 * me + q]
    g.remote_dma_fused([_fold(topo, [(NB + s) * 8 + 4 + q % 2], 1 << e, T.sem.fs, srcs, piece)
                        for e, s in enumerate(others)]
                       + [_fold(topo, [ranks[r]], 0xF00 << (4 * r), T.sem.ns, srcs, piece) for r in range(2)],
                       local_sem=T.sem.sent)
    sent += 5 + 8
    for b in order:
        g.wait_ge(T.sem["fb%d" % b], 4)
        piece = T.YB[4 * b + q]
        g.remote_dma_fused([_copy(topo, [ranks[r]], 0xFF << (8 * r), T.sem["nb%d" % b], piece, piece)
                            for r in range(2)], local_sem=T.sem.sent)
        sent += 16
    g.wait_ge(T.sem.sent, sent)


def _passer(g, core, T, topo):
    ch, i = topo.chip(core), core % 8 - 4
    me = ch - NB
    pieces = [4 * s + q for s in range(NS) if s != me for q in (i, i + 2)]
    g.wait_ge(T.sem.fs, 10)
    g.remote_dma_fused([_copy(topo, [ch * 8, ch * 8 + 1], 1 << e, T.sem.ns, T.YS[n], T.YS[n])
                        for e, n in enumerate(pieces)], local_sem=T.sem.sent)
    g.wait_ge(T.sem.sent, 10)


def _owner(g, core, T, topo):
    b, k = topo.chip(core), core % 8
    q = PORTS.index(k)
    srcs = [T.PB[s] for s in range(NS)]
    piece = T.YB[4 * b + q]
    g.wait_ge(T.sem.pb, 6 * 8)
    g.remote_dma_fused([_fold(topo, [c * 8 + k for c in range(NB, NB + NS) if (c + b + par) % 2 == 1],
                              0xF << (4 * par), T.sem["fb%d" % b], srcs, piece) for par in range(2)],
                       local_sem=T.sem.sent)
    g.wait_ge(T.sem.sent, 8)


def rank_program(g, core, T, topo):
    ch, k = topo.chip(core), core % 8
    if T.rank_of(core) is not None:
        _rank(g, core, T, topo)
    elif ch < NB:
        if k in PORTS:
            _owner(g, core, T, topo)
    elif k in PORTS:
        _port(g, core, T, topo)
    else:
        _passer(g, core, T, topo)
